import numpy as np
import ml_dtypes


def mxq(x, axis, fmt="e4m3"):
    dtype, down = {"e4m3": (ml_dtypes.float8_e4m3fn, 7), "e5m2": (ml_dtypes.float8_e5m2, 14)}[fmt]
    v = np.moveaxis(np.asarray(x, np.float32).astype(ml_dtypes.bfloat16).astype(np.float64), axis, -1)
    blocks = v.reshape(v.shape[:-1] + (-1, 32))
    amax = np.abs(blocks).max(-1, keepdims=True)
    byte = np.maximum(np.where(amax > 0, np.frexp(amax)[1] - 1 + 127, 0) - down, 1)
    scale = np.exp2(byte - 127.0)
    codes = (blocks / scale).astype(np.float32).astype(dtype).astype(np.float64)
    return np.moveaxis((codes * scale).reshape(v.shape), -1, axis)


WIDE = False


def mx_kscale(k):
    if not WIDE:
        return np.ones(k)
    levels = np.array([10, -10, 5, -5, 0])
    if k % 512:
        return np.exp2(np.random.permutation(np.resize(levels, k // 32))).repeat(32)
    a = np.empty((k // 512, 16))
    for p in range(k // 512):
        a[p, :8] = np.random.permutation(np.resize(levels, 8))
        for g in range(8):
            far = levels[np.abs(levels - a[p, g]) >= 10]
            a[p, g + 8] = far[np.random.randint(len(far))]
    return np.exp2(a.ravel()).repeat(32)


def f64(x):
    return np.asarray(x).astype(np.float64)


def striped(idx):
    return np.tile(idx.reshape(-1, 16).T, (8, 1)).astype(np.uint16)


def unstriped(offs):
    return offs[:16].T.reshape(-1).astype(np.int64)


def relu2(v):
    return np.maximum(v, 0.0) ** 2


K, T, E, C, H, N = 512, 640, 20, 128, 512, 128
TOP = 4


def by_expert(wq, xq):
    return np.concatenate([wq[e].T @ xq[:, e * C:(e + 1) * C] for e in range(E)], axis=1)


def setup_inputs():
    n = np.random.standard_normal
    s = mx_kscale(K)[:, None]
    u = mx_kscale(H)
    deal = np.repeat(np.arange(E), C).reshape(TOP, T)[:, np.random.permutation(T)]
    deal = np.take_along_axis(deal, np.argsort(np.random.rand(TOP, T), axis=0), axis=0)
    for _ in range(8):
        s_, t_ = np.random.permutation(T).reshape(2, -1); r = np.random.randint(TOP, size=T // 2); x, y = deal[r, s_].copy(), deal[r, t_].copy()
        ok = ~((deal[:, s_] == y).any(0) | (deal[:, t_] == x).any(0)); deal[r[ok], s_[ok]] = y[ok]; deal[r[ok], t_[ok]] = x[ok]
    order = np.lexsort((np.random.rand(TOP * T), deal.reshape(-1)))
    slot_token = order % T; pos = np.empty(TOP * T, np.int64); pos[order] = np.arange(TOP * T); pos = pos.reshape(TOP, T)
    g = np.random.uniform(0.5, 1.5, (TOP, T)); g = g / g.sum(0)
    w_slot = np.empty(E * C)
    for r in range(TOP): w_slot[pos[r]] = g[r]
    return {
        "xT": (n((K, T)) * s).astype(np.float32),
        "w1": (n((E, K, H)) / np.sqrt(K) / s[None] * u[None, None, :]).astype(np.float32),
        "w2": (n((E, H, N)) / np.sqrt(H) / u[None, :, None] ** 2).astype(np.float32),
        "gate": np.tile(w_slot, (K, 1)).astype(np.float32),
        "offs": striped(slot_token),
        "pos1": striped(pos[0]),
        "pos2": striped(pos[1]),
        "pos3": striped(pos[2]),
        "pos4": striped(pos[3]),
    }


def reference(xT, w1, w2, gate, offs, pos1, pos2, pos3, pos4):
    idx = unstriped(offs)
    xq = mxq(f64(gate) * f64(xT)[:, idx], 0, "e4m3")
    h = relu2(by_expert(mxq(f64(w1), 1, "e4m3"), xq))
    y = by_expert(mxq(f64(w2), 1, "e4m3"), mxq(h, 0, "e4m3"))
    return y[:, unstriped(pos1)] + y[:, unstriped(pos2)] + y[:, unstriped(pos3)] + y[:, unstriped(pos4)]

@@ -1,0 +1,259 @@
+from contextlib import ExitStack
+
+import concourse.mybir as mybir
+
+K, T, E, C, H, N = 512, 640, 20, 128, 512, 128
+S = E * C
+P = 128
+PACK = 4
+GROUP = 4
+GROUPS = E // GROUP
+GS = GROUP * C
+HALF = T // 2
+
+FLOPS = 2 * S * (K * H + H * N)
+BYTES = 4 * (K * T + E * K * H + E * H * N + S + N * T) + 2 * 128 * (S // 16 + 4 * T // 16)
+
+F32 = mybir.dt.float32
+BF16 = mybir.dt.bfloat16
+U32 = mybir.dt.uint32
+U16 = mybir.dt.uint16
+U8 = mybir.dt.uint8
+FP8X4 = mybir.dt.float8_e4m3fn_x4
+ACT = mybir.ActivationFunctionType
+ALU = mybir.AluOpType
+
+PAIRS = E // 2
+PS = 2 * C
+SCALAR_W1 = (0, 1, 2, 4, 6, 8, 10, 12, 14, 16, 18)
+RELU_LAG = 2
+H_LAG = 2
+W2_LAG = 2
+X_LEAD = 1
+RAW_BUFS = 9
+BF_BUFS = 3
+CODE_BUFS = 6
+XF_BUFS = 4
+HEAD = ("x0", "g0", "g1", "x1", "w0", "x2", "x3", "g2", "g3", "w1")
+GATE_AT = {1: 4, 2: 5, 3: 6, 4: 7, 5: 8, 6: 9}
+
+
+def tile_moe_pre_mlp_relu2_kernel(tc, xT, w1, w2, gate, offs, pos1, pos2, pos3, pos4, out):
+    nc = tc.nc
+    with ExitStack() as ctx:
+        lists = ctx.enter_context(tc.tile_pool(name="lists", bufs=1))
+        held = ctx.enter_context(tc.tile_pool(name="held", bufs=1))
+        raw = ctx.enter_context(tc.tile_pool(name="raw", bufs=RAW_BUFS))
+        raw2 = ctx.enter_context(tc.tile_pool(name="raw2", bufs=4))
+        xf = ctx.enter_context(tc.tile_pool(name="xf", bufs=XF_BUFS))
+        bfp = ctx.enter_context(tc.tile_pool(name="bfp", bufs=BF_BUFS))
+        mxp = ctx.enter_context(tc.tile_pool(name="mxp", bufs=CODE_BUFS))
+        psum_a = ctx.enter_context(tc.psum_pool(name="psum_a", bufs=5))
+        psum_y = ctx.enter_context(tc.psum_pool(name="psum_y", bufs=3))
+
+        offs_sb = lists.tile([P, S // 16], U16, name="offs_sb")
+        pos_sb = [lists.tile([P, T // 16], U16, name="pos_sb%d" % r) for r in range(4)]
+        x_win = [held.tile([P, T], F32, name="x_win%d" % t) for t in range(PACK)]
+        gate_sb = held.tile([P, S], F32, name="gate_sb")
+        y_sb = held.tile([P, S], F32, name="y_sb")
+        x_rows = xT.rearrange("(p j) c -> p j c", j=PACK)
+
+        WORDS = {"w1": H, "x": PS, "w2": 2 * N, "h": C}
+        calls = {}
+        for p in range(PAIRS):
+            calls["a", p] = [("w1", 2 * p), ("w1", 2 * p + 1)]
+        calls["x", 0] = [("x", 0), ("x", 1)]
+        for p in range(PAIRS + W2_LAG):
+            call = []
+            if 0 <= p - W2_LAG < PAIRS:
+                call.append(("w2", p - W2_LAG))
+            if 0 <= p - H_LAG < PAIRS:
+                call.extend([("h", 2 * (p - H_LAG)), ("h", 2 * (p - H_LAG) + 1)])
+            if p % 2 == X_LEAD % 2 and 0 < p + X_LEAD < PAIRS:
+                call.extend([("x", p + X_LEAD), ("x", p + X_LEAD + 1)])
+            if call:
+                calls["b", p] = call
+        place = {}
+        for c, call in calls.items():
+            start = 0
+            for operand in call:
+                place[operand] = (c, start)
+                start += WORDS[operand[0]]
+        bf_tiles, mx_tiles = {}, {}
+
+        def bf_of(operand):
+            c, start = place[operand]
+            if c not in bf_tiles:
+                width = sum(WORDS[o[0]] for o in calls[c])
+                bf_tiles[c] = bfp.tile([P, width * PACK], BF16, name="bf", tag="bf_" + c[0], align_bytes=64, bufs=1 if c[0] == "x" else BF_BUFS)
+            return bf_tiles[c][:, start * PACK:(start + WORDS[operand[0]]) * PACK]
+
+        def quantise(c):
+            width = sum(WORDS[o[0]] for o in calls[c])
+            bufs = {"a": 2, "b": 4, "x": 1}[c[0]]
+            codes = mxp.tile([P, width], U32, name="codes" + c[0], tag="codes_" + c[0], align_bytes=64, bufs=bufs)
+            scales = mxp.tile([P, width], U8, name="scales", tag="scales_" + c[0], align_bytes=64, bufs=bufs)
+            nc.vector.quantize_mx(out=codes[:].bitcast(FP8X4), scales=scales[:], in_=bf_tiles[c][:])
+            mx_tiles[c] = (codes, scales)
+
+        def mx_of(operand, first, count):
+            c, start = place[operand]
+            codes, scales = mx_tiles[c]
+            cols = slice(start + first, start + first + count)
+            return codes[:, cols].bitcast(FP8X4), scales[:, cols]
+
+        def load_gate(p):
+            cols = slice(p * PS, (p + 1) * PS)
+            nc.sync.dma_start(gate_sb[:, cols], gate[0:P, cols])
+
+        w1_raw, w2_raw, x_f32, a_ps, r_f32 = {}, {}, {}, {}, {}
+
+        def load_w1(e):
+            w1_raw[e] = raw.tile([P, PACK, H], F32, name="w_raw", tag="w_raw")
+            nc.sync.dma_start(w1_raw[e][:], w1[e].rearrange("(p j) c -> p j c", j=PACK))
+
+        def load_w2(p):
+            w2_raw[p] = raw2.tile([P, 2, PACK * N], F32, name="w2_raw", tag="w2_raw")
+            nc.sync.dma_start(w2_raw[p][:], w2[2 * p:2 * p + 2].rearrange("e (p j) n -> p e (j n)", j=PACK))
+
+        def gather_x(p):
+            x_f32[p] = xf.tile([P, PACK, PS], F32, name="x_f32")
+            for t in range(PACK):
+                nc.vector.tensor_tensor(
+                    x_f32[p][:, t, :],
+                    x_win[t][:].indirect(offs_sb[:, p * PS // 16:(p + 1) * PS // 16]),
+                    gate_sb[:, p * PS:(p + 1) * PS],
+                    ALU.mult,
+                )
+
+        def round_x(p):
+            nc.scalar.activation(
+                bf_of(("x", p)).rearrange("p (c i t) -> p c t i", i=4, t=PACK),
+                x_f32[p][:].rearrange("p t (c i) -> p c t i", i=4),
+                ACT.Copy,
+            )
+
+        def round_w1(e):
+            dst = bf_of(("w1", e)).rearrange("p (t m j) -> p m j t", t=PACK, j=PACK)
+            src = w1_raw[e][:].rearrange("p j (m t) -> p m j t", t=PACK)
+            if e in SCALAR_W1:
+                nc.scalar.activation(dst, src, ACT.Copy)
+            else:
+                nc.vector.tensor_copy(dst, src)
+
+        def round_w2(p):
+            for u in range(2):
+                nc.vector.tensor_copy(
+                    bf_of(("w2", p))[:, u * N * PACK:(u + 1) * N * PACK].rearrange("p (c i j) -> p c j i", i=4, j=PACK),
+                    w2_raw[p][:, u, :].rearrange("p (j c i) -> p c j i", i=4, j=PACK),
+                )
+
+        def layer1(e):
+            a_ps[e] = psum_a.tile([P, PACK, C], F32, name="a_ps")
+            x_codes, x_scales = mx_of(("x", e // 2), (e % 2) * C, C)
+            for t in range(PACK):
+                w_codes, w_scales = mx_of(("w1", e), t * P, P)
+                nc.tensor.matmul_mx(out=a_ps[e][:, t, :], lhsT=w_codes, lhsT_scale=w_scales, rhs=x_codes, rhs_scale=x_scales, start=True, stop=True)
+
+        spare = held.tile([P, 4, H], F32, name="spare")
+
+        def relu(e):
+            later = (e | 1) + RELU_LAG
+            r_f32[e] = w1_raw[later][:, e % 2, :] if later < E else spare[:, e % 4, :]
+            nc.scalar.activation(r_f32[e].rearrange("p (c t) -> p c t", t=PACK), a_ps[e][:].rearrange("p t c -> p c t"), ACT.Relu)
+
+        def square(e):
+            nc.scalar.activation(bf_of(("h", e)), r_f32[e], ACT.Square)
+
+        def layer2(p):
+            y_ps = psum_y.tile([P, PS], F32, name="y_ps", tag="y_ps")
+            for u in range(2):
+                w_codes, w_scales = mx_of(("w2", p), u * N, N)
+                h_codes, h_scales = mx_of(("h", 2 * p + u), 0, C)
+                nc.tensor.matmul_mx(out=y_ps[:, u * C:(u + 1) * C], lhsT=w_codes, lhsT_scale=w_scales, rhs=h_codes, rhs_scale=h_scales, start=True, stop=True)
+            nc.scalar.activation(y_sb[:, p * PS:(p + 1) * PS], y_ps[:], ACT.Copy)
+
+        nc.sync.dma_start(offs_sb[:], offs)
+        gate_step = {}
+        for item in HEAD:
+            kind, index = item[0], int(item[1])
+            if kind == "x":
+                nc.sync.dma_start(x_win[index][:], x_rows[:, index, :])
+            elif kind == "g":
+                load_gate(index)
+                gate_step[index] = 0
+            else:
+                load_w1(index)
+        for p in range(1, PAIRS + W2_LAG):
+            if p < PAIRS:
+                load_w1(2 * p)
+                load_w1(2 * p + 1)
+            if p in GATE_AT:
+                load_gate(GATE_AT[p])
+                gate_step[GATE_AT[p]] = p
+            if 0 <= p - W2_LAG:
+                load_w2(p - W2_LAG)
+        for r, pos in enumerate((pos1, pos2, pos3, pos4)):
+            nc.sync.dma_start(pos_sb[r][:], pos)
+
+        rounded = set()
+        for p in range(PAIRS + W2_LAG):
+            if p < PAIRS:
+                round_w1(2 * p)
+                round_w1(2 * p + 1)
+            for q in range(PAIRS):
+                if gate_step[q] == p:
+                    gather_x(q)
+            if p == 0:
+                round_x(0)
+                round_x(1)
+                rounded.add(0)
+                rounded.add(1)
+                quantise(("x", 0))
+            if 0 <= p - W2_LAG:
+                round_w2(p - W2_LAG)
+            if 0 <= p - 1 < PAIRS:
+                relu(2 * p - 2)
+                relu(2 * p - 1)
+                square(2 * p - 2)
+                square(2 * p - 1)
+            for q in range(PAIRS):
+                if gate_step[q] <= p and q not in rounded and place["x", q][0][1] <= p + 1:
+                    round_x(q)
+                    rounded.add(q)
+            if p < PAIRS:
+                quantise(("a", p))
+            if ("b", p) in calls:
+                quantise(("b", p))
+            if p < PAIRS:
+                layer1(2 * p)
+                layer1(2 * p + 1)
+            if 0 <= p - max(W2_LAG, H_LAG):
+                layer2(p - max(W2_LAG, H_LAG))
+
+        picked = [raw.tile([P, 4, HALF], F32, name="picked", tag="w_raw") for a in range(2)]
+        sums = [raw.tile([P, 3, HALF], F32, name="sums", tag="w_raw") for a in range(2)]
+
+        def pick(a, r):
+            nc.vector.tensor_copy(picked[a][:, r, :], y_sb[:].indirect(pos_sb[r][:, a * HALF // 16:(a + 1) * HALF // 16]))
+
+        def add(a, r):
+            so_far = picked[a][:, 0, :] if r == 1 else sums[a][:, r - 2, :]
+            nc.vector.tensor_tensor(sums[a][:, r - 1, :], so_far, picked[a][:, r, :], ALU.add)
+            if r == 3:
+                nc.sync.dma_start(out[:, a * HALF:(a + 1) * HALF], sums[a][:, 2, :])
+
+        pick(0, 0)
+        pick(0, 1)
+        pick(0, 2)
+        add(0, 1)
+        pick(0, 3)
+        add(0, 2)
+        pick(1, 0)
+        add(0, 3)
+        pick(1, 1)
+        pick(1, 2)
+        add(1, 1)
+        pick(1, 3)
+        add(1, 2)
+        add(1, 3)

@@ -25,17 +25,22 @@ ALU = mybir.AluOpType
 
 PAIRS = E // 2
 PS = 2 * C
-SCALAR_W1 = (0, 1, 2, 4, 6, 8, 10, 12, 14, 16, 18)
-RELU_LAG = 2
-H_LAG = 2
-W2_LAG = 2
-X_LEAD = 1
-RAW_BUFS = 9
-BF_BUFS = 3
-CODE_BUFS = 6
-XF_BUFS = 4
-HEAD = ("x0", "g0", "g1", "x1", "w0", "x2", "x3", "g2", "g3", "w1")
-GATE_AT = {1: 4, 2: 5, 3: 6, 4: 7, 5: 8, 6: 9}
+SCALAR_W1 = (0, 2, 4, 6, 8, 10, 12, 14, 16, 18)
+SCALAR_W2 = (0, 1, 2, 3, 4)
+W2_LOAD = (3, 4, 5, 6, 7, 8, 10, 10, 10, 10)
+W2_CALLS = ((0, 1), (2, 3), (4, 5), (6, 7), (8, 9))
+ODD_BUFS = 6
+EVEN_BUFS = 4
+BFA = 3
+BFC = 2
+MXA = 2
+MXB = 6
+MXC = 2
+W2_BUFS = 4
+HEAD = ("x0", "g0", "x1", "x2", "x3", "w1", "g1", "w0")
+FIRST = 1
+H_BF, X_BF, PLANES, RELU, WORK = 0, 512, 1024, 2048, 3072
+W1_AT = 768
 
 
 def tile_moe_pre_mlp_relu2_kernel(tc, xT, w1, w2, gate, offs, pos1, pos2, pos3, pos4, out):
@@ -43,11 +48,10 @@ def tile_moe_pre_mlp_relu2_kernel(tc, xT, w1, w2, gate, offs, pos1, pos2, pos3, 
     with ExitStack() as ctx:
         lists = ctx.enter_context(tc.tile_pool(name="lists", bufs=1))
         held = ctx.enter_context(tc.tile_pool(name="held", bufs=1))
-        raw = ctx.enter_context(tc.tile_pool(name="raw", bufs=RAW_BUFS))
-        raw2 = ctx.enter_context(tc.tile_pool(name="raw2", bufs=4))
-        xf = ctx.enter_context(tc.tile_pool(name="xf", bufs=XF_BUFS))
-        bfp = ctx.enter_context(tc.tile_pool(name="bfp", bufs=BF_BUFS))
-        mxp = ctx.enter_context(tc.tile_pool(name="mxp", bufs=CODE_BUFS))
+        raw = ctx.enter_context(tc.tile_pool(name="raw", bufs=1))
+        raw2 = ctx.enter_context(tc.tile_pool(name="raw2", bufs=W2_BUFS))
+        bfp = ctx.enter_context(tc.tile_pool(name="bfp", bufs=1))
+        mxp = ctx.enter_context(tc.tile_pool(name="mxp", bufs=1))
         psum_a = ctx.enter_context(tc.psum_pool(name="psum_a", bufs=5))
         psum_y = ctx.enter_context(tc.psum_pool(name="psum_y", bufs=3))
 
@@ -62,17 +66,15 @@ def tile_moe_pre_mlp_relu2_kernel(tc, xT, w1, w2, gate, offs, pos1, pos2, pos3, 
         calls = {}
         for p in range(PAIRS):
             calls["a", p] = [("w1", 2 * p), ("w1", 2 * p + 1)]
-        calls["x", 0] = [("x", 0), ("x", 1)]
-        for p in range(PAIRS + W2_LAG):
-            call = []
-            if 0 <= p - W2_LAG < PAIRS:
-                call.append(("w2", p - W2_LAG))
-            if 0 <= p - H_LAG < PAIRS:
-                call.extend([("h", 2 * (p - H_LAG)), ("h", 2 * (p - H_LAG) + 1)])
-            if p % 2 == X_LEAD % 2 and 0 < p + X_LEAD < PAIRS:
-                call.extend([("x", p + X_LEAD), ("x", p + X_LEAD + 1)])
-            if call:
-                calls["b", p] = call
+        for p in range(FIRST):
+            calls["x", p] = [("x", p)]
+        for p in range(PAIRS + 1):
+            call = [("h", 2 * p - 2), ("h", 2 * p - 1)] if p > 0 else []
+            if p + FIRST < PAIRS:
+                call.append(("x", p + FIRST))
+            calls["b", p] = call
+        for i, group in enumerate(W2_CALLS):
+            calls["c", i] = [("w2", q) for q in group]
         place = {}
         for c, call in calls.items():
             start = 0
@@ -81,19 +83,30 @@ def tile_moe_pre_mlp_relu2_kernel(tc, xT, w1, w2, gate, offs, pos1, pos2, pos3, 
                 start += WORDS[operand[0]]
         bf_tiles, mx_tiles = {}, {}
 
+        x_head = held.tile([P, FIRST + 1, PACK, PS], F32, name="x_head")
+        x_bf_own = held.tile([P, FIRST, PS * PACK], BF16, name="x_bf_own", align_bytes=64)
+
+        work = {}
+
         def bf_of(operand):
             c, start = place[operand]
             if c not in bf_tiles:
                 width = sum(WORDS[o[0]] for o in calls[c])
-                bf_tiles[c] = bfp.tile([P, width * PACK], BF16, name="bf", tag="bf_" + c[0], align_bytes=64, bufs=1 if c[0] == "x" else BF_BUFS)
+                if c[0] == "x":
+                    bf_tiles[c] = x_bf_own[:, c[1], :]
+                elif c[0] == "b":
+                    first = H_BF if c[1] > 0 else X_BF
+                    bf_tiles[c] = work[c[1]][:, first:first + 2 * width].bitcast(BF16)
+                else:
+                    bf_tiles[c] = bfp.tile([P, width * PACK], BF16, name="bf", tag="bf_" + c[0], align_bytes=64, bufs={"a": BFA, "c": BFC}[c[0]])[:]
             return bf_tiles[c][:, start * PACK:(start + WORDS[operand[0]]) * PACK]
 
         def quantise(c):
             width = sum(WORDS[o[0]] for o in calls[c])
-            bufs = {"a": 2, "b": 4, "x": 1}[c[0]]
+            bufs = {"a": MXA, "b": MXB, "c": MXC, "x": FIRST}[c[0]]
             codes = mxp.tile([P, width], U32, name="codes" + c[0], tag="codes_" + c[0], align_bytes=64, bufs=bufs)
             scales = mxp.tile([P, width], U8, name="scales", tag="scales_" + c[0], align_bytes=64, bufs=bufs)
-            nc.vector.quantize_mx(out=codes[:].bitcast(FP8X4), scales=scales[:], in_=bf_tiles[c][:])
+            nc.vector.quantize_mx(out=codes[:].bitcast(FP8X4), scales=scales[:], in_=bf_tiles[c])
             mx_tiles[c] = (codes, scales)
 
         def mx_of(operand, first, count):
@@ -109,44 +122,60 @@ def tile_moe_pre_mlp_relu2_kernel(tc, xT, w1, w2, gate, offs, pos1, pos2, pos3, 
         w1_raw, w2_raw, x_f32, a_ps, r_f32 = {}, {}, {}, {}, {}
 
         def load_w1(e):
-            w1_raw[e] = raw.tile([P, PACK, H], F32, name="w_raw", tag="w_raw")
-            nc.sync.dma_start(w1_raw[e][:], w1[e].rearrange("(p j) c -> p j c", j=PACK))
+            if e % 2:
+                work[e // 2] = raw.tile([P, WORK], F32, name="work", tag="work", align_bytes=64, bufs=ODD_BUFS)
+                w1_raw[e] = work[e // 2][:, W1_AT:W1_AT + PACK * H].rearrange("p (j c) -> p j c", j=PACK)
+            else:
+                w1_raw[e] = raw.tile([P, PACK, H], F32, name="w_raw", tag="w_raw", bufs=EVEN_BUFS)[:]
+            nc.sync.dma_start(w1_raw[e], w1[e].rearrange("(p j) c -> p j c", j=PACK))
 
         def load_w2(p):
             w2_raw[p] = raw2.tile([P, 2, PACK * N], F32, name="w2_raw", tag="w2_raw")
             nc.sync.dma_start(w2_raw[p][:], w2[2 * p:2 * p + 2].rearrange("e (p j) n -> p e (j n)", j=PACK))
 
         def gather_x(p):
-            x_f32[p] = xf.tile([P, PACK, PS], F32, name="x_f32")
+            if p <= FIRST:
+                x_f32[p] = x_head[:, p, :, :]
+            else:
+                x_f32[p] = work[p - FIRST - 1][:, PLANES:RELU].rearrange("p (t c) -> p t c", t=PACK)
             for t in range(PACK):
-                nc.vector.tensor_tensor(
-                    x_f32[p][:, t, :],
-                    x_win[t][:].indirect(offs_sb[:, p * PS // 16:(p + 1) * PS // 16]),
-                    gate_sb[:, p * PS:(p + 1) * PS],
+                window = x_win[t][:].indirect(offs_sb[:, p * PS // 16:(p + 1) * PS // 16])
+                if p < FIRST:
+                    nc.vector.tensor_tensor(x_f32[p][:, t, :], window, gate_sb[:, p * PS:(p + 1) * PS], ALU.mult)
+                else:
+                    nc.vector.tensor_copy(x_f32[p][:, t, :], window)
+
+        def round_x(p):
+            if p < FIRST:
+                nc.scalar.activation(
+                    bf_of(("x", p)).rearrange("p (c i t) -> p c t i", i=4, t=PACK),
+                    x_f32[p].rearrange("p t (c i) -> p c t i", i=4),
+                    ACT.Copy,
+                )
+            else:
+                engine = nc.vector if p == PAIRS - 1 else nc.gpsimd
+                engine.tensor_tensor(
+                    bf_of(("x", p)).rearrange("p (c t) -> p c t", t=PACK),
+                    x_f32[p].rearrange("p t c -> p c t"),
+                    gate_sb[:, p * PS:(p + 1) * PS].unsqueeze(2).to_broadcast([P, PS, PACK]),
                     ALU.mult,
                 )
 
-        def round_x(p):
-            nc.scalar.activation(
-                bf_of(("x", p)).rearrange("p (c i t) -> p c t i", i=4, t=PACK),
-                x_f32[p][:].rearrange("p t (c i) -> p c t i", i=4),
-                ACT.Copy,
-            )
-
         def round_w1(e):
             dst = bf_of(("w1", e)).rearrange("p (t m j) -> p m j t", t=PACK, j=PACK)
-            src = w1_raw[e][:].rearrange("p j (m t) -> p m j t", t=PACK)
+            src = w1_raw[e].rearrange("p j (m t) -> p m j t", t=PACK)
             if e in SCALAR_W1:
                 nc.scalar.activation(dst, src, ACT.Copy)
             else:
                 nc.vector.tensor_copy(dst, src)
 
         def round_w2(p):
-            for u in range(2):
-                nc.vector.tensor_copy(
-                    bf_of(("w2", p))[:, u * N * PACK:(u + 1) * N * PACK].rearrange("p (c i j) -> p c j i", i=4, j=PACK),
-                    w2_raw[p][:, u, :].rearrange("p (j c i) -> p c j i", i=4, j=PACK),
-                )
+            dst = bf_of(("w2", p)).rearrange("p (u c i j) -> p u c j i", u=2, i=4, j=PACK)
+            src = w2_raw[p][:].rearrange("p u (j c i) -> p u c j i", i=4, j=PACK)
+            if p in SCALAR_W2:
+                nc.scalar.copy(dst, src)
+            else:
+                nc.vector.tensor_copy(dst, src)
 
         def layer1(e):
             a_ps[e] = psum_a.tile([P, PACK, C], F32, name="a_ps")
@@ -155,11 +184,8 @@ def tile_moe_pre_mlp_relu2_kernel(tc, xT, w1, w2, gate, offs, pos1, pos2, pos3, 
                 w_codes, w_scales = mx_of(("w1", e), t * P, P)
                 nc.tensor.matmul_mx(out=a_ps[e][:, t, :], lhsT=w_codes, lhsT_scale=w_scales, rhs=x_codes, rhs_scale=x_scales, start=True, stop=True)
 
-        spare = held.tile([P, 4, H], F32, name="spare")
-
         def relu(e):
-            later = (e | 1) + RELU_LAG
-            r_f32[e] = w1_raw[later][:, e % 2, :] if later < E else spare[:, e % 4, :]
+            r_f32[e] = work[e // 2 + 1][:, RELU + (e % 2) * H:RELU + (e % 2 + 1) * H]
             nc.scalar.activation(r_f32[e].rearrange("p (c t) -> p c t", t=PACK), a_ps[e][:].rearrange("p t c -> p c t"), ACT.Relu)
 
         def square(e):
@@ -174,65 +200,73 @@ def tile_moe_pre_mlp_relu2_kernel(tc, xT, w1, w2, gate, offs, pos1, pos2, pos3, 
             nc.scalar.activation(y_sb[:, p * PS:(p + 1) * PS], y_ps[:], ACT.Copy)
 
         nc.sync.dma_start(offs_sb[:], offs)
-        gate_step = {}
         for item in HEAD:
             kind, index = item[0], int(item[1])
             if kind == "x":
                 nc.sync.dma_start(x_win[index][:], x_rows[:, index, :])
             elif kind == "g":
                 load_gate(index)
-                gate_step[index] = 0
             else:
                 load_w1(index)
-        for p in range(1, PAIRS + W2_LAG):
+        for p in range(1, PAIRS + 1):
             if p < PAIRS:
                 load_w1(2 * p)
                 load_w1(2 * p + 1)
-            if p in GATE_AT:
-                load_gate(GATE_AT[p])
-                gate_step[GATE_AT[p]] = p
-            if 0 <= p - W2_LAG:
-                load_w2(p - W2_LAG)
+            if p + FIRST < PAIRS:
+                load_gate(p + FIRST)
+            for q in range(PAIRS):
+                if W2_LOAD[q] == p:
+                    load_w2(q)
         for r, pos in enumerate((pos1, pos2, pos3, pos4)):
             nc.sync.dma_start(pos_sb[r][:], pos)
+        work[PAIRS] = raw.tile([P, WORK], F32, name="work", tag="work", align_bytes=64, bufs=ODD_BUFS)
 
-        rounded = set()
-        for p in range(PAIRS + W2_LAG):
+        for q in range(FIRST + 1):
+            gather_x(q)
+        for q in range(FIRST):
+            round_x(q)
+            quantise(("x", q))
+        finished = 0
+        for p in range(PAIRS + 1):
             if p < PAIRS:
-                round_w1(2 * p)
                 round_w1(2 * p + 1)
-            for q in range(PAIRS):
-                if gate_step[q] == p:
-                    gather_x(q)
-            if p == 0:
-                round_x(0)
-                round_x(1)
-                rounded.add(0)
-                rounded.add(1)
-                quantise(("x", 0))
-            if 0 <= p - W2_LAG:
-                round_w2(p - W2_LAG)
-            if 0 <= p - 1 < PAIRS:
+                round_w1(2 * p)
+            if p + FIRST + 1 < PAIRS:
+                gather_x(p + FIRST + 1)
+            if p + FIRST < PAIRS:
+                round_x(p + FIRST)
+            if p > 0:
                 relu(2 * p - 2)
                 relu(2 * p - 1)
                 square(2 * p - 2)
                 square(2 * p - 1)
-            for q in range(PAIRS):
-                if gate_step[q] <= p and q not in rounded and place["x", q][0][1] <= p + 1:
-                    round_x(q)
-                    rounded.add(q)
+            arrived = [q for q in range(PAIRS) if W2_LOAD[q] == p]
             if p < PAIRS:
+                for q in arrived:
+                    round_w2(q)
                 quantise(("a", p))
-            if ("b", p) in calls:
-                quantise(("b", p))
+            else:
+                round_w2(arrived[0])
+            for i, group in enumerate(W2_CALLS):
+                if W2_LOAD[group[-1]] == p:
+                    if p == PAIRS:
+                        for q in group:
+                            if q != arrived[0]:
+                                round_w2(q)
+                    if p < PAIRS or i < len(W2_CALLS) - 1:
+                        quantise(("c", i))
+            quantise(("b", p))
+            if p == PAIRS:
+                quantise(("c", len(W2_CALLS) - 1))
             if p < PAIRS:
                 layer1(2 * p)
                 layer1(2 * p + 1)
-            if 0 <= p - max(W2_LAG, H_LAG):
-                layer2(p - max(W2_LAG, H_LAG))
+            while finished < p and place["w2", finished][0] in mx_tiles:
+                layer2(finished)
+                finished += 1
 
-        picked = [raw.tile([P, 4, HALF], F32, name="picked", tag="w_raw") for a in range(2)]
-        sums = [raw.tile([P, 3, HALF], F32, name="sums", tag="w_raw") for a in range(2)]
+        picked = [raw.tile([P, 4, HALF], F32, name="picked", tag="w_raw", bufs=EVEN_BUFS) for a in range(2)]
+        sums = [raw.tile([P, 3, HALF], F32, name="sums", tag="w_raw", bufs=EVEN_BUFS) for a in range(2)]
 
         def pick(a, r):
             nc.vector.tensor_copy(picked[a][:, r, :], y_sb[:].indirect(pos_sb[r][:, a * HALF // 16:(a + 1) * HALF // 16]))

@@ -26,19 +26,24 @@ ALU = mybir.AluOpType
 PAIRS = E // 2
 PS = 2 * C
 SCALAR_W1 = (0, 2, 4, 6, 8, 10, 12, 14, 16, 18)
-SCALAR_W2 = (0, 1, 2, 3, 4)
-W2_LOAD = (3, 4, 5, 6, 7, 8, 10, 10, 10, 10)
-W2_CALLS = ((0, 1), (2, 3), (4, 5), (6, 7), (8, 9))
+SCALAR_W2 = (0, 1, 3, 4, 8)
+W2_LOAD = (2, 3, 4, 5, 6, 7, 8, 10, 10, 10)
+W2_CALLS = ((0, 1, 2, 3), (4, 5), (6, 7), (8, 9))
 ODD_BUFS = 6
 EVEN_BUFS = 4
 BFA = 3
 BFC = 2
 MXA = 2
-MXB = 6
+MXB = 5
 MXC = 2
 W2_BUFS = 4
 HEAD = ("x0", "g0", "x1", "x2", "x3", "w1", "g1", "w0")
 FIRST = 1
+POOL_SLOTS = 208
+VECTOR_RELU = (16, 18)
+VECTOR_SQUARE = ()
+SPLIT = (1, 3, 5, 7, 9, 11, 13, 15)
+SHARE = {1: 32}
 H_BF, X_BF, PLANES, RELU, WORK = 0, 512, 1024, 2048, 3072
 W1_AT = 768
 
@@ -66,10 +71,8 @@ def tile_moe_pre_mlp_relu2_kernel(tc, xT, w1, w2, gate, offs, pos1, pos2, pos3, 
         calls = {}
         for p in range(PAIRS):
             calls["a", p] = [("w1", 2 * p), ("w1", 2 * p + 1)]
-        for p in range(FIRST):
-            calls["x", p] = [("x", p)]
         for p in range(PAIRS + 1):
-            call = [("h", 2 * p - 2), ("h", 2 * p - 1)] if p > 0 else []
+            call = [("h", 2 * p - 2), ("h", 2 * p - 1)] if p > 0 else [("x", 0)]
             if p + FIRST < PAIRS:
                 call.append(("x", p + FIRST))
             calls["b", p] = call
@@ -84,7 +87,6 @@ def tile_moe_pre_mlp_relu2_kernel(tc, xT, w1, w2, gate, offs, pos1, pos2, pos3, 
         bf_tiles, mx_tiles = {}, {}
 
         x_head = held.tile([P, FIRST + 1, PACK, PS], F32, name="x_head")
-        x_bf_own = held.tile([P, FIRST, PS * PACK], BF16, name="x_bf_own", align_bytes=64)
 
         work = {}
 
@@ -92,18 +94,15 @@ def tile_moe_pre_mlp_relu2_kernel(tc, xT, w1, w2, gate, offs, pos1, pos2, pos3, 
             c, start = place[operand]
             if c not in bf_tiles:
                 width = sum(WORDS[o[0]] for o in calls[c])
-                if c[0] == "x":
-                    bf_tiles[c] = x_bf_own[:, c[1], :]
-                elif c[0] == "b":
-                    first = H_BF if c[1] > 0 else X_BF
-                    bf_tiles[c] = work[c[1]][:, first:first + 2 * width].bitcast(BF16)
+                if c[0] == "b":
+                    bf_tiles[c] = work[c[1]][:, H_BF:H_BF + 2 * width].bitcast(BF16)
                 else:
                     bf_tiles[c] = bfp.tile([P, width * PACK], BF16, name="bf", tag="bf_" + c[0], align_bytes=64, bufs={"a": BFA, "c": BFC}[c[0]])[:]
             return bf_tiles[c][:, start * PACK:(start + WORDS[operand[0]]) * PACK]
 
         def quantise(c):
             width = sum(WORDS[o[0]] for o in calls[c])
-            bufs = {"a": MXA, "b": MXB, "c": MXC, "x": FIRST}[c[0]]
+            bufs = {"a": MXA, "b": MXB, "c": MXC}[c[0]]
             codes = mxp.tile([P, width], U32, name="codes" + c[0], tag="codes_" + c[0], align_bytes=64, bufs=bufs)
             scales = mxp.tile([P, width], U8, name="scales", tag="scales_" + c[0], align_bytes=64, bufs=bufs)
             nc.vector.quantize_mx(out=codes[:].bitcast(FP8X4), scales=scales[:], in_=bf_tiles[c])
@@ -153,19 +152,27 @@ def tile_moe_pre_mlp_relu2_kernel(tc, xT, w1, w2, gate, offs, pos1, pos2, pos3, 
                     ACT.Copy,
                 )
             else:
-                engine = nc.vector if p == PAIRS - 1 else nc.gpsimd
-                engine.tensor_tensor(
-                    bf_of(("x", p)).rearrange("p (c t) -> p c t", t=PACK),
-                    x_f32[p].rearrange("p t c -> p c t"),
-                    gate_sb[:, p * PS:(p + 1) * PS].unsqueeze(2).to_broadcast([P, PS, PACK]),
-                    ALU.mult,
-                )
+                cut = 0 if p == PAIRS - 1 else POOL_SLOTS
+                for engine, lo, hi in ((nc.gpsimd, 0, cut), (nc.vector, cut, PS)):
+                    if lo < hi:
+                        engine.tensor_tensor(
+                            bf_of(("x", p)).rearrange("p (c t) -> p c t", t=PACK)[:, lo:hi, :],
+                            x_f32[p].rearrange("p t c -> p c t")[:, lo:hi, :],
+                            gate_sb[:, p * PS + lo:p * PS + hi].unsqueeze(2).to_broadcast([P, hi - lo, PACK]),
+                            ALU.mult,
+                        )
 
         def round_w1(e):
             dst = bf_of(("w1", e)).rearrange("p (t m j) -> p m j t", t=PACK, j=PACK)
             src = w1_raw[e].rearrange("p j (m t) -> p m j t", t=PACK)
-            if e in SCALAR_W1:
+            if e in SHARE:
+                nc.scalar.activation(dst[:, :SHARE[e]], src[:, :SHARE[e]], ACT.Copy)
+                nc.vector.tensor_copy(dst[:, SHARE[e]:], src[:, SHARE[e]:])
+            elif e in SCALAR_W1:
                 nc.scalar.activation(dst, src, ACT.Copy)
+            elif e in SPLIT:
+                nc.vector.tensor_copy(dst[:, :P // 2], src[:, :P // 2])
+                nc.vector.tensor_copy(dst[:, P // 2:], src[:, P // 2:])
             else:
                 nc.vector.tensor_copy(dst, src)
 
@@ -186,10 +193,17 @@ def tile_moe_pre_mlp_relu2_kernel(tc, xT, w1, w2, gate, offs, pos1, pos2, pos3, 
 
         def relu(e):
             r_f32[e] = work[e // 2 + 1][:, RELU + (e % 2) * H:RELU + (e % 2 + 1) * H]
-            nc.scalar.activation(r_f32[e].rearrange("p (c t) -> p c t", t=PACK), a_ps[e][:].rearrange("p t c -> p c t"), ACT.Relu)
+            dst, src = r_f32[e].rearrange("p (c t) -> p c t", t=PACK), a_ps[e][:].rearrange("p t c -> p c t")
+            if e in VECTOR_RELU:
+                nc.vector.tensor_scalar(dst, src, 0.0, None, ALU.max)
+            else:
+                nc.scalar.activation(dst, src, ACT.Relu)
 
         def square(e):
-            nc.scalar.activation(bf_of(("h", e)), r_f32[e], ACT.Square)
+            if e in VECTOR_SQUARE:
+                nc.vector.tensor_tensor(bf_of(("h", e)), r_f32[e], r_f32[e], ALU.mult)
+            else:
+                nc.scalar.activation(bf_of(("h", e)), r_f32[e], ACT.Square)
 
         def layer2(p):
             y_ps = psum_y.tile([P, PS], F32, name="y_ps", tag="y_ps")
@@ -225,7 +239,6 @@ def tile_moe_pre_mlp_relu2_kernel(tc, xT, w1, w2, gate, offs, pos1, pos2, pos3, 
             gather_x(q)
         for q in range(FIRST):
             round_x(q)
-            quantise(("x", q))
         finished = 0
         for p in range(PAIRS + 1):
             if p < PAIRS:
@@ -235,29 +248,23 @@ def tile_moe_pre_mlp_relu2_kernel(tc, xT, w1, w2, gate, offs, pos1, pos2, pos3, 
                 gather_x(p + FIRST + 1)
             if p + FIRST < PAIRS:
                 round_x(p + FIRST)
+            arrived = [q for q in range(PAIRS) if W2_LOAD[q] == p]
             if p > 0:
                 relu(2 * p - 2)
                 relu(2 * p - 1)
+            if p == PAIRS:
+                round_w2(arrived.pop(0))
+            if p > 0:
                 square(2 * p - 2)
                 square(2 * p - 1)
-            arrived = [q for q in range(PAIRS) if W2_LOAD[q] == p]
+            for q in arrived:
+                round_w2(q)
             if p < PAIRS:
-                for q in arrived:
-                    round_w2(q)
                 quantise(("a", p))
-            else:
-                round_w2(arrived[0])
             for i, group in enumerate(W2_CALLS):
                 if W2_LOAD[group[-1]] == p:
-                    if p == PAIRS:
-                        for q in group:
-                            if q != arrived[0]:
-                                round_w2(q)
-                    if p < PAIRS or i < len(W2_CALLS) - 1:
-                        quantise(("c", i))
+                    quantise(("c", i))
             quantise(("b", p))
-            if p == PAIRS:
-                quantise(("c", len(W2_CALLS) - 1))
             if p < PAIRS:
                 layer1(2 * p)
                 layer1(2 * p + 1)
@@ -267,27 +274,13 @@ def tile_moe_pre_mlp_relu2_kernel(tc, xT, w1, w2, gate, offs, pos1, pos2, pos3, 
 
         picked = [raw.tile([P, 4, HALF], F32, name="picked", tag="w_raw", bufs=EVEN_BUFS) for a in range(2)]
         sums = [raw.tile([P, 3, HALF], F32, name="sums", tag="w_raw", bufs=EVEN_BUFS) for a in range(2)]
-
-        def pick(a, r):
-            nc.vector.tensor_copy(picked[a][:, r, :], y_sb[:].indirect(pos_sb[r][:, a * HALF // 16:(a + 1) * HALF // 16]))
-
-        def add(a, r):
-            so_far = picked[a][:, 0, :] if r == 1 else sums[a][:, r - 2, :]
-            nc.vector.tensor_tensor(sums[a][:, r - 1, :], so_far, picked[a][:, r, :], ALU.add)
-            if r == 3:
-                nc.sync.dma_start(out[:, a * HALF:(a + 1) * HALF], sums[a][:, 2, :])
-
-        pick(0, 0)
-        pick(0, 1)
-        pick(0, 2)
-        add(0, 1)
-        pick(0, 3)
-        add(0, 2)
-        pick(1, 0)
-        add(0, 3)
-        pick(1, 1)
-        pick(1, 2)
-        add(1, 1)
-        pick(1, 3)
-        add(1, 2)
-        add(1, 3)
+        for a in range(2):
+            for r in range(4):
+                nc.vector.tensor_copy(picked[a][:, r, :], y_sb[:].indirect(pos_sb[r][:, a * HALF // 16:(a + 1) * HALF // 16]))
+        nc.gpsimd.tensor_tensor(sums[0][:, 0:2, :], picked[0][:, 0:2, :], picked[0][:, 2:4, :], ALU.add)
+        nc.gpsimd.tensor_tensor(sums[0][:, 2, :], sums[0][:, 0, :], sums[0][:, 1, :], ALU.add)
+        nc.scalar.dma_start(out[:, :HALF], sums[0][:, 2, :])
+        nc.vector.tensor_tensor(sums[1][:, 0, :], picked[1][:, 0, :], picked[1][:, 1, :], ALU.add)
+        nc.vector.tensor_tensor(sums[1][:, 1, :], picked[1][:, 2, :], picked[1][:, 3, :], ALU.add)
+        nc.vector.tensor_tensor(sums[1][:, 2, :], sums[1][:, 0, :], sums[1][:, 1, :], ALU.add)
+        nc.sync.dma_start(out[:, HALF:], sums[1][:, 2, :])

@@ -6,13 +6,14 @@ K, T, E, C, H, N = 512, 640, 20, 128, 512, 128
 S = E * C
 P = 128
 PACK = 4
-GROUP = 4
-GROUPS = E // GROUP
-GS = GROUP * C
+LINE = 4
+PER_COLUMN = 16
+PAIRS = E // 2
+PS = 2 * C
 HALF = T // 2
 
 FLOPS = 2 * S * (K * H + H * N)
-BYTES = 4 * (K * T + E * K * H + E * H * N + S + N * T) + 2 * 128 * (S // 16 + 4 * T // 16)
+BYTES = 4 * (K * T + E * K * H + E * H * N + S + N * T) + 2 * P * (S + 4 * T) // PER_COLUMN
 
 F32 = mybir.dt.float32
 BF16 = mybir.dt.bfloat16
@@ -23,29 +24,21 @@ FP8X4 = mybir.dt.float8_e4m3fn_x4
 ACT = mybir.ActivationFunctionType
 ALU = mybir.AluOpType
 
-PAIRS = E // 2
-PS = 2 * C
-SCALAR_W1 = (0, 2, 4, 6, 8, 10, 12, 14, 16, 18)
-SCALAR_W2 = (0, 1, 3, 4, 8)
-W2_LOAD = (2, 3, 4, 5, 6, 7, 8, 10, 10, 10)
-W2_CALLS = ((0, 1, 2, 3), (4, 5), (6, 7), (8, 9))
-ODD_BUFS = 6
-EVEN_BUFS = 4
-BFA = 3
-BFC = 2
-MXA = 2
-MXB = 5
-MXC = 2
-W2_BUFS = 4
-HEAD = ("x0", "g0", "x1", "x2", "x3", "w1", "g1", "w0")
-FIRST = 1
-POOL_SLOTS = 208
-VECTOR_RELU = (16, 18)
-VECTOR_SQUARE = ()
-SPLIT = (1, 3, 5, 7, 9, 11, 13, 15)
-SHARE = {1: 32}
-H_BF, X_BF, PLANES, RELU, WORK = 0, 512, 1024, 2048, 3072
+W2_STEP = (2, 3, 4, 5, 6, 7, PAIRS, PAIRS, PAIRS, PAIRS)
+W2_CALLS = ((0, 1), (2, 3), (4, 5), (6, 7), (8,), (9,))
+SCALAR_W2 = (0, 1, 2, 3, 4, 5, 7)
+SHARED_W1, SCALAR_SHARE = (3, 5), 32
+VECTOR_RELU = 16
+
+H_AND_X, PLANES, RELU, WORK = 0, 1024, 2048, 3072
 W1_AT = 768
+
+WORK_BUFS, EVEN_BUFS, W2_BUFS = 6, 4, 4
+ROUNDED_BUFS = {"w1": 3, "w2": 2}
+CODE_BUFS = {"w1": 2, "hx": 6, "w2": 2}
+A_BANKS, Y_BANKS = 5, 3
+
+WORDS = {"w1": H, "x": PS, "w2": 2 * N, "h": C}
 
 
 def tile_moe_pre_mlp_relu2_kernel(tc, xT, w1, w2, gate, offs, pos1, pos2, pos3, pos4, out):
@@ -55,200 +48,197 @@ def tile_moe_pre_mlp_relu2_kernel(tc, xT, w1, w2, gate, offs, pos1, pos2, pos3, 
         held = ctx.enter_context(tc.tile_pool(name="held", bufs=1))
         raw = ctx.enter_context(tc.tile_pool(name="raw", bufs=1))
         raw2 = ctx.enter_context(tc.tile_pool(name="raw2", bufs=W2_BUFS))
-        bfp = ctx.enter_context(tc.tile_pool(name="bfp", bufs=1))
-        mxp = ctx.enter_context(tc.tile_pool(name="mxp", bufs=1))
-        psum_a = ctx.enter_context(tc.psum_pool(name="psum_a", bufs=5))
-        psum_y = ctx.enter_context(tc.psum_pool(name="psum_y", bufs=3))
+        rounded = ctx.enter_context(tc.tile_pool(name="rounded", bufs=1))
+        quantised = ctx.enter_context(tc.tile_pool(name="quantised", bufs=1))
+        psum_a = ctx.enter_context(tc.psum_pool(name="psum_a", bufs=A_BANKS))
+        psum_y = ctx.enter_context(tc.psum_pool(name="psum_y", bufs=Y_BANKS))
 
-        offs_sb = lists.tile([P, S // 16], U16, name="offs_sb")
-        pos_sb = [lists.tile([P, T // 16], U16, name="pos_sb%d" % r) for r in range(4)]
-        x_win = [held.tile([P, T], F32, name="x_win%d" % t) for t in range(PACK)]
+        offs_sb = lists.tile([P, S // PER_COLUMN], U16, name="offs_sb")
+        pos_sb = [lists.tile([P, T // PER_COLUMN], U16, name="pos_sb%d" % r) for r in range(4)]
+        x_plane = [held.tile([P, T], F32, name="x_plane%d" % t) for t in range(PACK)]
         gate_sb = held.tile([P, S], F32, name="gate_sb")
         y_sb = held.tile([P, S], F32, name="y_sb")
-        x_rows = xT.rearrange("(p j) c -> p j c", j=PACK)
+        x_first = held.tile([P, 2, PACK, PS], F32, name="x_first")
 
-        WORDS = {"w1": H, "x": PS, "w2": 2 * N, "h": C}
         calls = {}
         for p in range(PAIRS):
-            calls["a", p] = [("w1", 2 * p), ("w1", 2 * p + 1)]
+            calls["w1", p] = [("w1", 2 * p), ("w1", 2 * p + 1)]
         for p in range(PAIRS + 1):
-            call = [("h", 2 * p - 2), ("h", 2 * p - 1)] if p > 0 else [("x", 0)]
-            if p + FIRST < PAIRS:
-                call.append(("x", p + FIRST))
-            calls["b", p] = call
-        for i, group in enumerate(W2_CALLS):
-            calls["c", i] = [("w2", q) for q in group]
+            calls["hx", p] = [("h", 2 * p - 2), ("h", 2 * p - 1)] if p > 0 else [("x", 0)]
+            if p + 1 < PAIRS:
+                calls["hx", p].append(("x", p + 1))
+        for number, pairs in enumerate(W2_CALLS):
+            calls["w2", number] = [("w2", q) for q in pairs]
         place = {}
-        for c, call in calls.items():
+        for call, operands in calls.items():
             start = 0
-            for operand in call:
-                place[operand] = (c, start)
+            for operand in operands:
+                place[operand] = (call, start)
                 start += WORDS[operand[0]]
-        bf_tiles, mx_tiles = {}, {}
 
-        x_head = held.tile([P, FIRST + 1, PACK, PS], F32, name="x_head")
+        work, w1_raw, w2_raw, x_f32, a_ps = {}, {}, {}, {}, {}
+        call_input, call_output = {}, {}
 
-        work = {}
+        def call_words(call):
+            return sum(WORDS[kind] for kind, index in calls[call])
 
-        def bf_of(operand):
-            c, start = place[operand]
-            if c not in bf_tiles:
-                width = sum(WORDS[o[0]] for o in calls[c])
-                if c[0] == "b":
-                    bf_tiles[c] = work[c[1]][:, H_BF:H_BF + 2 * width].bitcast(BF16)
+        def bf16_of(operand):
+            call, start = place[operand]
+            kind, number = call
+            if call not in call_input:
+                if kind == "hx":
+                    call_input[call] = work[number][:, H_AND_X:H_AND_X + 2 * call_words(call)].bitcast(BF16)
                 else:
-                    bf_tiles[c] = bfp.tile([P, width * PACK], BF16, name="bf", tag="bf_" + c[0], align_bytes=64, bufs={"a": BFA, "c": BFC}[c[0]])[:]
-            return bf_tiles[c][:, start * PACK:(start + WORDS[operand[0]]) * PACK]
+                    values = rounded.tile([P, call_words(call) * PACK], BF16, name="values", tag=kind, align_bytes=64, bufs=ROUNDED_BUFS[kind])
+                    call_input[call] = values[:]
+            return call_input[call][:, start * PACK:(start + WORDS[operand[0]]) * PACK]
 
-        def quantise(c):
-            width = sum(WORDS[o[0]] for o in calls[c])
-            bufs = {"a": MXA, "b": MXB, "c": MXC}[c[0]]
-            codes = mxp.tile([P, width], U32, name="codes" + c[0], tag="codes_" + c[0], align_bytes=64, bufs=bufs)
-            scales = mxp.tile([P, width], U8, name="scales", tag="scales_" + c[0], align_bytes=64, bufs=bufs)
-            nc.vector.quantize_mx(out=codes[:].bitcast(FP8X4), scales=scales[:], in_=bf_tiles[c])
-            mx_tiles[c] = (codes, scales)
+        def quantise(call):
+            kind = call[0]
+            codes = quantised.tile([P, call_words(call)], U32, name="codes", tag="codes_" + kind, align_bytes=64, bufs=CODE_BUFS[kind])
+            scales = quantised.tile([P, call_words(call)], U8, name="scales", tag="scales_" + kind, align_bytes=64, bufs=CODE_BUFS[kind])
+            nc.vector.quantize_mx(out=codes[:].bitcast(FP8X4), scales=scales[:], in_=call_input[call])
+            call_output[call] = (codes, scales)
 
-        def mx_of(operand, first, count):
-            c, start = place[operand]
-            codes, scales = mx_tiles[c]
-            cols = slice(start + first, start + first + count)
-            return codes[:, cols].bitcast(FP8X4), scales[:, cols]
+        def multiply(result, stationary, stationary_first, moving, moving_first):
+            views = []
+            for operand, first in ((stationary, stationary_first), (moving, moving_first)):
+                call, start = place[operand]
+                codes, scales = call_output[call]
+                columns = slice(start + first, start + first + P)
+                views.append((codes[:, columns].bitcast(FP8X4), scales[:, columns]))
+            nc.tensor.matmul_mx(
+                out=result, lhsT=views[0][0], lhsT_scale=views[0][1], rhs=views[1][0], rhs_scale=views[1][1], start=True, stop=True
+            )
+
+        def slots(p):
+            return slice(p * PS, (p + 1) * PS)
+
+        def load_x_plane(t):
+            nc.sync.dma_start(x_plane[t][:], xT.rearrange("(p j) c -> p j c", j=PACK)[:, t, :])
 
         def load_gate(p):
-            cols = slice(p * PS, (p + 1) * PS)
-            nc.sync.dma_start(gate_sb[:, cols], gate[0:P, cols])
-
-        w1_raw, w2_raw, x_f32, a_ps, r_f32 = {}, {}, {}, {}, {}
+            nc.sync.dma_start(gate_sb[:, slots(p)], gate[0:P, slots(p)])
 
         def load_w1(e):
             if e % 2:
-                work[e // 2] = raw.tile([P, WORK], F32, name="work", tag="work", align_bytes=64, bufs=ODD_BUFS)
+                work[e // 2] = raw.tile([P, WORK], F32, name="work", tag="work", align_bytes=64, bufs=WORK_BUFS)
                 w1_raw[e] = work[e // 2][:, W1_AT:W1_AT + PACK * H].rearrange("p (j c) -> p j c", j=PACK)
             else:
-                w1_raw[e] = raw.tile([P, PACK, H], F32, name="w_raw", tag="w_raw", bufs=EVEN_BUFS)[:]
+                even = raw.tile([P, PACK, H], F32, name="even", tag="even", bufs=EVEN_BUFS)
+                w1_raw[e] = even[:]
             nc.sync.dma_start(w1_raw[e], w1[e].rearrange("(p j) c -> p j c", j=PACK))
 
-        def load_w2(p):
-            w2_raw[p] = raw2.tile([P, 2, PACK * N], F32, name="w2_raw", tag="w2_raw")
-            nc.sync.dma_start(w2_raw[p][:], w2[2 * p:2 * p + 2].rearrange("e (p j) n -> p e (j n)", j=PACK))
+        def load_w2(q):
+            w2_raw[q] = raw2.tile([P, 2, PACK * N], F32, name="w2_raw")
+            nc.sync.dma_start(w2_raw[q][:], w2[2 * q:2 * q + 2].rearrange("e (p j) n -> p e (j n)", j=PACK))
 
         def gather_x(p):
-            if p <= FIRST:
-                x_f32[p] = x_head[:, p, :, :]
-            else:
-                x_f32[p] = work[p - FIRST - 1][:, PLANES:RELU].rearrange("p (t c) -> p t c", t=PACK)
+            x_f32[p] = x_first[:, p, :, :] if p < 2 else work[p - 2][:, PLANES:RELU].rearrange("p (t c) -> p t c", t=PACK)
             for t in range(PACK):
-                window = x_win[t][:].indirect(offs_sb[:, p * PS // 16:(p + 1) * PS // 16])
-                if p < FIRST:
-                    nc.vector.tensor_tensor(x_f32[p][:, t, :], window, gate_sb[:, p * PS:(p + 1) * PS], ALU.mult)
+                window = x_plane[t][:].indirect(offs_sb[:, p * PS // PER_COLUMN:(p + 1) * PS // PER_COLUMN])
+                if p == 0:
+                    nc.vector.tensor_tensor(x_f32[p][:, t, :], window, gate_sb[:, slots(p)], ALU.mult)
                 else:
                     nc.vector.tensor_copy(x_f32[p][:, t, :], window)
 
         def round_x(p):
-            if p < FIRST:
-                nc.scalar.activation(
-                    bf_of(("x", p)).rearrange("p (c i t) -> p c t i", i=4, t=PACK),
-                    x_f32[p].rearrange("p t (c i) -> p c t i", i=4),
-                    ACT.Copy,
-                )
+            values = bf16_of(("x", p))
+            if p in (0, PAIRS - 1):
+                dst = values.rearrange("p (c i t) -> p c t i", i=LINE, t=PACK)
+                src = x_f32[p].rearrange("p t (c i) -> p c t i", i=LINE)
+                if p == 0:
+                    nc.scalar.activation(dst, src, ACT.Copy)
+                else:
+                    weights = gate_sb[:, slots(p)].rearrange("p (c i) -> p c i", i=LINE)
+                    nc.vector.tensor_tensor(dst, src, weights.unsqueeze(2).to_broadcast([P, PS // LINE, PACK, LINE]), ALU.mult)
             else:
-                cut = 0 if p == PAIRS - 1 else POOL_SLOTS
-                for engine, lo, hi in ((nc.gpsimd, 0, cut), (nc.vector, cut, PS)):
-                    if lo < hi:
-                        engine.tensor_tensor(
-                            bf_of(("x", p)).rearrange("p (c t) -> p c t", t=PACK)[:, lo:hi, :],
-                            x_f32[p].rearrange("p t c -> p c t")[:, lo:hi, :],
-                            gate_sb[:, p * PS + lo:p * PS + hi].unsqueeze(2).to_broadcast([P, hi - lo, PACK]),
-                            ALU.mult,
-                        )
+                nc.gpsimd.tensor_tensor(
+                    values.rearrange("p (c t) -> p c t", t=PACK),
+                    x_f32[p].rearrange("p t c -> p c t"),
+                    gate_sb[:, slots(p)].unsqueeze(2).to_broadcast([P, PS, PACK]),
+                    ALU.mult,
+                )
 
         def round_w1(e):
-            dst = bf_of(("w1", e)).rearrange("p (t m j) -> p m j t", t=PACK, j=PACK)
+            dst = bf16_of(("w1", e)).rearrange("p (t m j) -> p m j t", t=PACK, j=PACK)
             src = w1_raw[e].rearrange("p j (m t) -> p m j t", t=PACK)
-            if e in SHARE:
-                nc.scalar.activation(dst[:, :SHARE[e]], src[:, :SHARE[e]], ACT.Copy)
-                nc.vector.tensor_copy(dst[:, SHARE[e]:], src[:, SHARE[e]:])
-            elif e in SCALAR_W1:
+            if e in SHARED_W1:
+                nc.scalar.activation(dst[:, :SCALAR_SHARE], src[:, :SCALAR_SHARE], ACT.Copy)
+                nc.vector.tensor_copy(dst[:, SCALAR_SHARE:], src[:, SCALAR_SHARE:])
+            elif e % 2 == 0:
                 nc.scalar.activation(dst, src, ACT.Copy)
-            elif e in SPLIT:
-                nc.vector.tensor_copy(dst[:, :P // 2], src[:, :P // 2])
-                nc.vector.tensor_copy(dst[:, P // 2:], src[:, P // 2:])
             else:
                 nc.vector.tensor_copy(dst, src)
 
-        def round_w2(p):
-            dst = bf_of(("w2", p)).rearrange("p (u c i j) -> p u c j i", u=2, i=4, j=PACK)
-            src = w2_raw[p][:].rearrange("p u (j c i) -> p u c j i", i=4, j=PACK)
-            if p in SCALAR_W2:
+        def round_w2(q):
+            dst = bf16_of(("w2", q)).rearrange("p (u c i j) -> p u c j i", u=2, i=LINE, j=PACK)
+            src = w2_raw[q][:].rearrange("p u (j c i) -> p u c j i", i=LINE, j=PACK)
+            if q in SCALAR_W2:
                 nc.scalar.copy(dst, src)
             else:
                 nc.vector.tensor_copy(dst, src)
 
-        def layer1(e):
+        def first_layer(e):
             a_ps[e] = psum_a.tile([P, PACK, C], F32, name="a_ps")
-            x_codes, x_scales = mx_of(("x", e // 2), (e % 2) * C, C)
             for t in range(PACK):
-                w_codes, w_scales = mx_of(("w1", e), t * P, P)
-                nc.tensor.matmul_mx(out=a_ps[e][:, t, :], lhsT=w_codes, lhsT_scale=w_scales, rhs=x_codes, rhs_scale=x_scales, start=True, stop=True)
+                multiply(a_ps[e][:, t, :], ("w1", e), t * P, ("x", e // 2), (e % 2) * C)
+
+        def relu_result(e):
+            first = RELU + (e % 2) * H
+            return work[e // 2 + 1][:, first:first + H]
 
         def relu(e):
-            r_f32[e] = work[e // 2 + 1][:, RELU + (e % 2) * H:RELU + (e % 2 + 1) * H]
-            dst, src = r_f32[e].rearrange("p (c t) -> p c t", t=PACK), a_ps[e][:].rearrange("p t c -> p c t")
-            if e in VECTOR_RELU:
+            dst = relu_result(e).rearrange("p (c t) -> p c t", t=PACK)
+            src = a_ps[e][:].rearrange("p t c -> p c t")
+            if e == VECTOR_RELU:
                 nc.vector.tensor_scalar(dst, src, 0.0, None, ALU.max)
             else:
                 nc.scalar.activation(dst, src, ACT.Relu)
 
         def square(e):
-            if e in VECTOR_SQUARE:
-                nc.vector.tensor_tensor(bf_of(("h", e)), r_f32[e], r_f32[e], ALU.mult)
-            else:
-                nc.scalar.activation(bf_of(("h", e)), r_f32[e], ACT.Square)
+            nc.scalar.activation(bf16_of(("h", e)), relu_result(e), ACT.Square)
 
-        def layer2(p):
-            y_ps = psum_y.tile([P, PS], F32, name="y_ps", tag="y_ps")
+        def second_layer(p):
+            y_ps = psum_y.tile([P, PS], F32, name="y_ps")
             for u in range(2):
-                w_codes, w_scales = mx_of(("w2", p), u * N, N)
-                h_codes, h_scales = mx_of(("h", 2 * p + u), 0, C)
-                nc.tensor.matmul_mx(out=y_ps[:, u * C:(u + 1) * C], lhsT=w_codes, lhsT_scale=w_scales, rhs=h_codes, rhs_scale=h_scales, start=True, stop=True)
-            nc.scalar.activation(y_sb[:, p * PS:(p + 1) * PS], y_ps[:], ACT.Copy)
+                multiply(y_ps[:, u * C:(u + 1) * C], ("w2", p), u * N, ("h", 2 * p + u), 0)
+            nc.scalar.activation(y_sb[:, slots(p)], y_ps[:], ACT.Copy)
 
         nc.sync.dma_start(offs_sb[:], offs)
-        for item in HEAD:
-            kind, index = item[0], int(item[1])
-            if kind == "x":
-                nc.sync.dma_start(x_win[index][:], x_rows[:, index, :])
-            elif kind == "g":
-                load_gate(index)
-            else:
-                load_w1(index)
+        load_x_plane(0)
+        load_gate(0)
+        for t in range(1, PACK):
+            load_x_plane(t)
+        load_w1(1)
+        load_gate(1)
+        load_w1(0)
         for p in range(1, PAIRS + 1):
             if p < PAIRS:
                 load_w1(2 * p)
                 load_w1(2 * p + 1)
-            if p + FIRST < PAIRS:
-                load_gate(p + FIRST)
+            if p + 1 < PAIRS:
+                load_gate(p + 1)
             for q in range(PAIRS):
-                if W2_LOAD[q] == p:
+                if W2_STEP[q] == p:
                     load_w2(q)
         for r, pos in enumerate((pos1, pos2, pos3, pos4)):
             nc.sync.dma_start(pos_sb[r][:], pos)
-        work[PAIRS] = raw.tile([P, WORK], F32, name="work", tag="work", align_bytes=64, bufs=ODD_BUFS)
+        work[PAIRS] = raw.tile([P, WORK], F32, name="work", tag="work", align_bytes=64, bufs=WORK_BUFS)
 
-        for q in range(FIRST + 1):
-            gather_x(q)
-        for q in range(FIRST):
-            round_x(q)
+        gather_x(0)
+        gather_x(1)
+        round_x(0)
         finished = 0
         for p in range(PAIRS + 1):
             if p < PAIRS:
                 round_w1(2 * p + 1)
                 round_w1(2 * p)
-            if p + FIRST + 1 < PAIRS:
-                gather_x(p + FIRST + 1)
-            if p + FIRST < PAIRS:
-                round_x(p + FIRST)
-            arrived = [q for q in range(PAIRS) if W2_LOAD[q] == p]
+            if p + 2 < PAIRS:
+                gather_x(p + 2)
+            if p + 1 < PAIRS:
+                round_x(p + 1)
+            arrived = [q for q in range(PAIRS) if W2_STEP[q] == p]
             if p > 0:
                 relu(2 * p - 2)
                 relu(2 * p - 1)
@@ -260,23 +250,24 @@ def tile_moe_pre_mlp_relu2_kernel(tc, xT, w1, w2, gate, offs, pos1, pos2, pos3, 
             for q in arrived:
                 round_w2(q)
             if p < PAIRS:
-                quantise(("a", p))
-            for i, group in enumerate(W2_CALLS):
-                if W2_LOAD[group[-1]] == p:
-                    quantise(("c", i))
-            quantise(("b", p))
+                quantise(("w1", p))
+            for number, pairs in enumerate(W2_CALLS):
+                if W2_STEP[pairs[-1]] == p:
+                    quantise(("w2", number))
+            quantise(("hx", p))
             if p < PAIRS:
-                layer1(2 * p)
-                layer1(2 * p + 1)
-            while finished < p and place["w2", finished][0] in mx_tiles:
-                layer2(finished)
+                first_layer(2 * p)
+                first_layer(2 * p + 1)
+            while finished < p and place["w2", finished][0] in call_output:
+                second_layer(finished)
                 finished += 1
 
-        picked = [raw.tile([P, 4, HALF], F32, name="picked", tag="w_raw", bufs=EVEN_BUFS) for a in range(2)]
-        sums = [raw.tile([P, 3, HALF], F32, name="sums", tag="w_raw", bufs=EVEN_BUFS) for a in range(2)]
-        for a in range(2):
+        picked = [raw.tile([P, 4, HALF], F32, name="picked", tag="even", bufs=EVEN_BUFS) for half in range(2)]
+        sums = [raw.tile([P, 3, HALF], F32, name="sums", tag="even", bufs=EVEN_BUFS) for half in range(2)]
+        for half in range(2):
+            entries = slice(half * HALF // PER_COLUMN, (half + 1) * HALF // PER_COLUMN)
             for r in range(4):
-                nc.vector.tensor_copy(picked[a][:, r, :], y_sb[:].indirect(pos_sb[r][:, a * HALF // 16:(a + 1) * HALF // 16]))
+                nc.vector.tensor_copy(picked[half][:, r, :], y_sb[:].indirect(pos_sb[r][:, entries]))
         nc.gpsimd.tensor_tensor(sums[0][:, 0:2, :], picked[0][:, 0:2, :], picked[0][:, 2:4, :], ALU.add)
         nc.gpsimd.tensor_tensor(sums[0][:, 2, :], sums[0][:, 0, :], sums[0][:, 1, :], ALU.add)
         nc.scalar.dma_start(out[:, :HALF], sums[0][:, 2, :])

from contextlib import ExitStack

import concourse.mybir as mybir

K, T, E, C, H, N = 512, 640, 20, 128, 512, 128
S = E * C
P = 128
PACK = 4
LINE = 4
PER_COLUMN = 16
PAIRS = E // 2
PS = 2 * C
HALF = T // 2

FLOPS = 2 * S * (K * H + H * N)
BYTES = 4 * (K * T + E * K * H + E * H * N + S + N * T) + 2 * P * (S + 4 * T) // PER_COLUMN

F32 = mybir.dt.float32
BF16 = mybir.dt.bfloat16
U32 = mybir.dt.uint32
U16 = mybir.dt.uint16
U8 = mybir.dt.uint8
FP8X4 = mybir.dt.float8_e4m3fn_x4
ACT = mybir.ActivationFunctionType
ALU = mybir.AluOpType

W2_STEP = (2, 3, 4, 5, 6, 7, PAIRS, PAIRS, PAIRS, PAIRS)
W2_CALLS = ((0, 1), (2, 3), (4, 5), (6, 7), (8,), (9,))
SCALAR_W2 = (0, 1, 2, 3, 4, 5, 7)
SHARED_W1, SCALAR_SHARE = (3, 5), 32
VECTOR_RELU = 16

H_AND_X, PLANES, RELU, WORK = 0, 1024, 2048, 3072
W1_AT = 768

WORK_BUFS, EVEN_BUFS, W2_BUFS = 6, 4, 4
ROUNDED_BUFS = {"w1": 3, "w2": 2}
CODE_BUFS = {"w1": 2, "hx": 6, "w2": 2}
A_BANKS, Y_BANKS = 5, 3

WORDS = {"w1": H, "x": PS, "w2": 2 * N, "h": C}


def tile_moe_pre_mlp_relu2_kernel(tc, xT, w1, w2, gate, offs, pos1, pos2, pos3, pos4, out):
    nc = tc.nc
    with ExitStack() as ctx:
        lists = ctx.enter_context(tc.tile_pool(name="lists", bufs=1))
        held = ctx.enter_context(tc.tile_pool(name="held", bufs=1))
        raw = ctx.enter_context(tc.tile_pool(name="raw", bufs=1))
        raw2 = ctx.enter_context(tc.tile_pool(name="raw2", bufs=W2_BUFS))
        rounded = ctx.enter_context(tc.tile_pool(name="rounded", bufs=1))
        quantised = ctx.enter_context(tc.tile_pool(name="quantised", bufs=1))
        psum_a = ctx.enter_context(tc.psum_pool(name="psum_a", bufs=A_BANKS))
        psum_y = ctx.enter_context(tc.psum_pool(name="psum_y", bufs=Y_BANKS))

        offs_sb = lists.tile([P, S // PER_COLUMN], U16, name="offs_sb")
        pos_sb = [lists.tile([P, T // PER_COLUMN], U16, name="pos_sb%d" % r) for r in range(4)]
        x_plane = [held.tile([P, T], F32, name="x_plane%d" % t) for t in range(PACK)]
        gate_sb = held.tile([P, S], F32, name="gate_sb")
        y_sb = held.tile([P, S], F32, name="y_sb")
        x_first = held.tile([P, 2, PACK, PS], F32, name="x_first")

        calls = {}
        for p in range(PAIRS):
            calls["w1", p] = [("w1", 2 * p), ("w1", 2 * p + 1)]
        for p in range(PAIRS + 1):
            calls["hx", p] = [("h", 2 * p - 2), ("h", 2 * p - 1)] if p > 0 else [("x", 0)]
            if p + 1 < PAIRS:
                calls["hx", p].append(("x", p + 1))
        for number, pairs in enumerate(W2_CALLS):
            calls["w2", number] = [("w2", q) for q in pairs]
        place = {}
        for call, operands in calls.items():
            start = 0
            for operand in operands:
                place[operand] = (call, start)
                start += WORDS[operand[0]]

        work, w1_raw, w2_raw, x_f32, a_ps = {}, {}, {}, {}, {}
        call_input, call_output = {}, {}

        def call_words(call):
            return sum(WORDS[kind] for kind, index in calls[call])

        def bf16_of(operand):
            call, start = place[operand]
            kind, number = call
            if call not in call_input:
                if kind == "hx":
                    call_input[call] = work[number][:, H_AND_X:H_AND_X + 2 * call_words(call)].bitcast(BF16)
                else:
                    values = rounded.tile([P, call_words(call) * PACK], BF16, name="values", tag=kind, align_bytes=64, bufs=ROUNDED_BUFS[kind])
                    call_input[call] = values[:]
            return call_input[call][:, start * PACK:(start + WORDS[operand[0]]) * PACK]

        def quantise(call):
            kind = call[0]
            codes = quantised.tile([P, call_words(call)], U32, name="codes", tag="codes_" + kind, align_bytes=64, bufs=CODE_BUFS[kind])
            scales = quantised.tile([P, call_words(call)], U8, name="scales", tag="scales_" + kind, align_bytes=64, bufs=CODE_BUFS[kind])
            nc.vector.quantize_mx(out=codes[:].bitcast(FP8X4), scales=scales[:], in_=call_input[call])
            call_output[call] = (codes, scales)

        def multiply(result, stationary, stationary_first, moving, moving_first):
            views = []
            for operand, first in ((stationary, stationary_first), (moving, moving_first)):
                call, start = place[operand]
                codes, scales = call_output[call]
                columns = slice(start + first, start + first + P)
                views.append((codes[:, columns].bitcast(FP8X4), scales[:, columns]))
            nc.tensor.matmul_mx(
                out=result, lhsT=views[0][0], lhsT_scale=views[0][1], rhs=views[1][0], rhs_scale=views[1][1], start=True, stop=True
            )

        def slots(p):
            return slice(p * PS, (p + 1) * PS)

        def load_x_plane(t):
            nc.sync.dma_start(x_plane[t][:], xT.rearrange("(p j) c -> p j c", j=PACK)[:, t, :])

        def load_gate(p):
            nc.sync.dma_start(gate_sb[:, slots(p)], gate[0:P, slots(p)])

        def load_w1(e):
            if e % 2:
                work[e // 2] = raw.tile([P, WORK], F32, name="work", tag="work", align_bytes=64, bufs=WORK_BUFS)
                w1_raw[e] = work[e // 2][:, W1_AT:W1_AT + PACK * H].rearrange("p (j c) -> p j c", j=PACK)
            else:
                even = raw.tile([P, PACK, H], F32, name="even", tag="even", bufs=EVEN_BUFS)
                w1_raw[e] = even[:]
            nc.sync.dma_start(w1_raw[e], w1[e].rearrange("(p j) c -> p j c", j=PACK))

        def load_w2(q):
            w2_raw[q] = raw2.tile([P, 2, PACK * N], F32, name="w2_raw")
            nc.sync.dma_start(w2_raw[q][:], w2[2 * q:2 * q + 2].rearrange("e (p j) n -> p e (j n)", j=PACK))

        def gather_x(p):
            x_f32[p] = x_first[:, p, :, :] if p < 2 else work[p - 2][:, PLANES:RELU].rearrange("p (t c) -> p t c", t=PACK)
            for t in range(PACK):
                window = x_plane[t][:].indirect(offs_sb[:, p * PS // PER_COLUMN:(p + 1) * PS // PER_COLUMN])
                if p == 0:
                    nc.vector.tensor_tensor(x_f32[p][:, t, :], window, gate_sb[:, slots(p)], ALU.mult)
                else:
                    nc.vector.tensor_copy(x_f32[p][:, t, :], window)

        def round_x(p):
            values = bf16_of(("x", p))
            if p in (0, PAIRS - 1):
                dst = values.rearrange("p (c i t) -> p c t i", i=LINE, t=PACK)
                src = x_f32[p].rearrange("p t (c i) -> p c t i", i=LINE)
                if p == 0:
                    nc.scalar.activation(dst, src, ACT.Copy)
                else:
                    weights = gate_sb[:, slots(p)].rearrange("p (c i) -> p c i", i=LINE)
                    nc.vector.tensor_tensor(dst, src, weights.unsqueeze(2).to_broadcast([P, PS // LINE, PACK, LINE]), ALU.mult)
            else:
                nc.gpsimd.tensor_tensor(
                    values.rearrange("p (c t) -> p c t", t=PACK),
                    x_f32[p].rearrange("p t c -> p c t"),
                    gate_sb[:, slots(p)].unsqueeze(2).to_broadcast([P, PS, PACK]),
                    ALU.mult,
                )

        def round_w1(e):
            dst = bf16_of(("w1", e)).rearrange("p (t m j) -> p m j t", t=PACK, j=PACK)
            src = w1_raw[e].rearrange("p j (m t) -> p m j t", t=PACK)
            if e in SHARED_W1:
                nc.scalar.activation(dst[:, :SCALAR_SHARE], src[:, :SCALAR_SHARE], ACT.Copy)
                nc.vector.tensor_copy(dst[:, SCALAR_SHARE:], src[:, SCALAR_SHARE:])
            elif e % 2 == 0:
                nc.scalar.activation(dst, src, ACT.Copy)
            else:
                nc.vector.tensor_copy(dst, src)

        def round_w2(q):
            dst = bf16_of(("w2", q)).rearrange("p (u c i j) -> p u c j i", u=2, i=LINE, j=PACK)
            src = w2_raw[q][:].rearrange("p u (j c i) -> p u c j i", i=LINE, j=PACK)
            if q in SCALAR_W2:
                nc.scalar.copy(dst, src)
            else:
                nc.vector.tensor_copy(dst, src)

        def first_layer(e):
            a_ps[e] = psum_a.tile([P, PACK, C], F32, name="a_ps")
            for t in range(PACK):
                multiply(a_ps[e][:, t, :], ("w1", e), t * P, ("x", e // 2), (e % 2) * C)

        def relu_result(e):
            first = RELU + (e % 2) * H
            return work[e // 2 + 1][:, first:first + H]

        def relu(e):
            dst = relu_result(e).rearrange("p (c t) -> p c t", t=PACK)
            src = a_ps[e][:].rearrange("p t c -> p c t")
            if e == VECTOR_RELU:
                nc.vector.tensor_scalar(dst, src, 0.0, None, ALU.max)
            else:
                nc.scalar.activation(dst, src, ACT.Relu)

        def square(e):
            nc.scalar.activation(bf16_of(("h", e)), relu_result(e), ACT.Square)

        def second_layer(p):
            y_ps = psum_y.tile([P, PS], F32, name="y_ps")
            for u in range(2):
                multiply(y_ps[:, u * C:(u + 1) * C], ("w2", p), u * N, ("h", 2 * p + u), 0)
            nc.scalar.activation(y_sb[:, slots(p)], y_ps[:], ACT.Copy)

        nc.sync.dma_start(offs_sb[:], offs)
        load_x_plane(0)
        load_gate(0)
        for t in range(1, PACK):
            load_x_plane(t)
        load_w1(1)
        load_gate(1)
        load_w1(0)
        for p in range(1, PAIRS + 1):
            if p < PAIRS:
                load_w1(2 * p)
                load_w1(2 * p + 1)
            if p + 1 < PAIRS:
                load_gate(p + 1)
            for q in range(PAIRS):
                if W2_STEP[q] == p:
                    load_w2(q)
        for r, pos in enumerate((pos1, pos2, pos3, pos4)):
            nc.sync.dma_start(pos_sb[r][:], pos)
        work[PAIRS] = raw.tile([P, WORK], F32, name="work", tag="work", align_bytes=64, bufs=WORK_BUFS)

        gather_x(0)
        gather_x(1)
        round_x(0)
        finished = 0
        for p in range(PAIRS + 1):
            if p < PAIRS:
                round_w1(2 * p + 1)
                round_w1(2 * p)
            if p + 2 < PAIRS:
                gather_x(p + 2)
            if p + 1 < PAIRS:
                round_x(p + 1)
            arrived = [q for q in range(PAIRS) if W2_STEP[q] == p]
            if p > 0:
                relu(2 * p - 2)
                relu(2 * p - 1)
            if p == PAIRS:
                round_w2(arrived.pop(0))
            if p > 0:
                square(2 * p - 2)
                square(2 * p - 1)
            for q in arrived:
                round_w2(q)
            if p < PAIRS:
                quantise(("w1", p))
            for number, pairs in enumerate(W2_CALLS):
                if W2_STEP[pairs[-1]] == p:
                    quantise(("w2", number))
            quantise(("hx", p))
            if p < PAIRS:
                first_layer(2 * p)
                first_layer(2 * p + 1)
            while finished < p and place["w2", finished][0] in call_output:
                second_layer(finished)
                finished += 1

        picked = [raw.tile([P, 4, HALF], F32, name="picked", tag="even", bufs=EVEN_BUFS) for half in range(2)]
        sums = [raw.tile([P, 3, HALF], F32, name="sums", tag="even", bufs=EVEN_BUFS) for half in range(2)]
        for half in range(2):
            entries = slice(half * HALF // PER_COLUMN, (half + 1) * HALF // PER_COLUMN)
            for r in range(4):
                nc.vector.tensor_copy(picked[half][:, r, :], y_sb[:].indirect(pos_sb[r][:, entries]))
        nc.gpsimd.tensor_tensor(sums[0][:, 0:2, :], picked[0][:, 0:2, :], picked[0][:, 2:4, :], ALU.add)
        nc.gpsimd.tensor_tensor(sums[0][:, 2, :], sums[0][:, 0, :], sums[0][:, 1, :], ALU.add)
        nc.scalar.dma_start(out[:, :HALF], sums[0][:, 2, :])
        nc.vector.tensor_tensor(sums[1][:, 0, :], picked[1][:, 0, :], picked[1][:, 1, :], ALU.add)
        nc.vector.tensor_tensor(sums[1][:, 1, :], picked[1][:, 2, :], picked[1][:, 3, :], ALU.add)
        nc.vector.tensor_tensor(sums[1][:, 2, :], sums[1][:, 0, :], sums[1][:, 1, :], ALU.add)
        nc.sync.dma_start(out[:, HALF:], sums[1][:, 2, :])
